import numpy as np
import ml_dtypes

BF16 = ml_dtypes.bfloat16


def bf(x):
    return np.asarray(x, np.float32).astype(BF16)


def f32(x):
    return np.asarray(x, np.float32)


def f64(x):
    return np.asarray(x).astype(np.float64)


def striped(idx):
    return np.tile(idx.reshape(-1, 16).T, (8, 1))


S, K, M, N, D, V = 512, 256, 128, 256, 4, 64


def setup_inputs():
    return {"table": bf(np.random.standard_normal((S, K))), "w": bf(np.random.standard_normal((D, K, M)) / np.sqrt(D * K)), "b": f32(0.5 * np.random.standard_normal((M, 1))), "offs": striped(np.random.permutation(S)[:N])}


def reference(table, w, b, offs):
    idx = offs[:16].T.reshape(-1)
    x = f64(table)[idx].T
    y = sum(f64(w)[t].T @ x[:, t * V : (t + 1) * V] for t in range(D))
    return np.tanh(y + f64(b))

@@ -1,0 +1,88 @@
+import concourse.mybir as mybir
+from concourse.masks import make_identity
+
+BF16, F32, U16 = mybir.dt.bfloat16, mybir.dt.float32, mybir.dt.uint16
+TANH = mybir.ActivationFunctionType.Tanh
+
+P = 128
+S, K, M = 512, 256, 128
+D, V = 4, 64
+ROW_BLOCKS = S // P
+K_BLOCKS = K // P
+PIECE_COLS = V // 16
+DMA_GRID = 256
+
+WARM_MATMULS = 3
+WARM_REPEATS = 4
+
+FLOPS = 2 * D * K * M * V
+
+
+def tile_gather_matmul_kernel(tc, table, w, b, offs, out):
+    nc = tc.nc
+    with (
+        tc.tile_pool(name="held", bufs=1) as held,
+        tc.psum_pool(name="psum", bufs=1) as psum,
+        tc.psum_pool(name="flips", bufs=6) as flips,
+    ):
+        rows = held.tile([P, ROW_BLOCKS, K], BF16, name="rows", align_bytes=DMA_GRID)
+        blocked = table.rearrange("(a p) k -> p a k", p=P)
+        half = ROW_BLOCKS // 2
+        nc.sync.dma_start(rows[:, :half, :], blocked[:, :half, :])
+        nc.scalar.dma_start(rows[:, half:, :], blocked[:, half:, :])
+
+        offsets = held.tile([P, D * PIECE_COLS], U16, name="offsets")
+        nc.sync.dma_start(offsets[:], offs)
+
+        weights = held.tile([P, D, K_BLOCKS, M], BF16, name="weights", align_bytes=DMA_GRID)
+        for t, queue in zip(range(0, D, 2), (nc.scalar, nc.sync)):
+            queue.dma_start(
+                weights[:, t : t + 2, :, :].rearrange("p t c m -> p t (c m)"),
+                w[t : t + 2].rearrange("t (p c) m -> p t (c m)", c=K_BLOCKS),
+            )
+
+        bias = held.tile([P, 1], F32, name="bias")
+        nc.sync.dma_start(bias[:], b)
+
+        identity = held.tile([P, P], BF16, name="identity")
+        make_identity(nc, identity[:])
+
+        zeros = held.tile([P, P], BF16, name="zeros")
+        nc.vector.memset(zeros[:], 0.0)
+        idle = psum.tile([P, WARM_REPEATS, P], F32, name="idle")
+        for i in range(WARM_MATMULS):
+            nc.tensor.matmul(
+                idle[:],
+                zeros[:],
+                zeros[:].unsqueeze(1).to_broadcast([P, WARM_REPEATS, P]),
+                start=True,
+                stop=True,
+            )
+
+        warm = held.tile([P, 1], F32, name="warm")
+        nc.vector.memset(warm[:], 0.0)
+        nc.scalar.activation(warm[:], warm[:], TANH)
+
+        features = [held.tile([P, S], BF16, name=f"features{c}") for c in range(K_BLOCKS)]
+        for c in range(K_BLOCKS):
+            for a in range(ROW_BLOCKS):
+                flipped = flips.tile([P, P], BF16, name="flipped")
+                nc.tensor.transpose(flipped[:], rows[:, a, c::K_BLOCKS], identity[:])
+                nc.vector.tensor_copy(features[c][:, a * P : (a + 1) * P], flipped[:])
+
+        acc = psum.tile([P, V], F32, name="acc")
+        steps = [(c, t) for c in range(K_BLOCKS) for t in range(D)]
+        for i, (c, t) in enumerate(steps):
+            piece = offsets[:, t * PIECE_COLS : (t + 1) * PIECE_COLS]
+            nc.tensor.matmul(
+                acc[:],
+                weights[:, t, c, :],
+                features[c][:].indirect(piece),
+                start=(i == 0),
+                stop=(i == len(steps) - 1),
+            )
+
+        result = held.tile([P, V], F32, name="result", align_bytes=DMA_GRID)
+        nc.scalar.activation(result[:], acc[:], TANH, bias=bias[:, 0:1])
+        for first in range(0, V, V // 2):
+            nc.scalar.dma_start(out[:, first : first + V // 2], result[:, first : first + V // 2])

@@ -23,7 +23,7 @@ def tile_gather_matmul_kernel(tc, table, w, b, offs, out):
     with (
         tc.tile_pool(name="held", bufs=1) as held,
         tc.psum_pool(name="psum", bufs=1) as psum,
-        tc.psum_pool(name="flips", bufs=6) as flips,
+        tc.psum_pool(name="flips", bufs=ROW_BLOCKS // 2 * K_BLOCKS) as flips,
     ):
         rows = held.tile([P, ROW_BLOCKS, K], BF16, name="rows", align_bytes=DMA_GRID)
         blocked = table.rearrange("(a p) k -> p a k", p=P)
@@ -65,10 +65,13 @@ def tile_gather_matmul_kernel(tc, table, w, b, offs, out):
 
         features = [held.tile([P, S], BF16, name=f"features{c}") for c in range(K_BLOCKS)]
         for c in range(K_BLOCKS):
-            for a in range(ROW_BLOCKS):
-                flipped = flips.tile([P, P], BF16, name="flipped")
-                nc.tensor.transpose(flipped[:], rows[:, a, c::K_BLOCKS], identity[:])
-                nc.vector.tensor_copy(features[c][:, a * P : (a + 1) * P], flipped[:])
+            for a in range(0, ROW_BLOCKS, 2):
+                flipped = flips.tile([P, 2, P], BF16, name="flipped")
+                for i in range(2):
+                    nc.tensor.transpose(flipped[:, i, :], rows[:, a + i, c::K_BLOCKS], identity[:])
+                nc.vector.tensor_copy(
+                    features[c][:, a * P : (a + 2) * P], flipped[:].rearrange("p i s -> p (i s)")
+                )
 
         acc = psum.tile([P, V], F32, name="acc")
         steps = [(c, t) for c in range(K_BLOCKS) for t in range(D)]

import concourse.mybir as mybir
from concourse.masks import make_identity

BF16, F32, U16 = mybir.dt.bfloat16, mybir.dt.float32, mybir.dt.uint16
TANH = mybir.ActivationFunctionType.Tanh

P = 128
S, K, M = 512, 256, 128
D, V = 4, 64
ROW_BLOCKS = S // P
K_BLOCKS = K // P
PIECE_COLS = V // 16
DMA_GRID = 256

WARM_MATMULS = 3
WARM_REPEATS = 4

FLOPS = 2 * D * K * M * V


def tile_gather_matmul_kernel(tc, table, w, b, offs, out):
    nc = tc.nc
    with (
        tc.tile_pool(name="held", bufs=1) as held,
        tc.psum_pool(name="psum", bufs=1) as psum,
        tc.psum_pool(name="flips", bufs=ROW_BLOCKS // 2 * K_BLOCKS) as flips,
    ):
        rows = held.tile([P, ROW_BLOCKS, K], BF16, name="rows", align_bytes=DMA_GRID)
        blocked = table.rearrange("(a p) k -> p a k", p=P)
        half = ROW_BLOCKS // 2
        nc.sync.dma_start(rows[:, :half, :], blocked[:, :half, :])
        nc.scalar.dma_start(rows[:, half:, :], blocked[:, half:, :])

        offsets = held.tile([P, D * PIECE_COLS], U16, name="offsets")
        nc.sync.dma_start(offsets[:], offs)

        weights = held.tile([P, D, K_BLOCKS, M], BF16, name="weights", align_bytes=DMA_GRID)
        for t, queue in zip(range(0, D, 2), (nc.scalar, nc.sync)):
            queue.dma_start(
                weights[:, t : t + 2, :, :].rearrange("p t c m -> p t (c m)"),
                w[t : t + 2].rearrange("t (p c) m -> p t (c m)", c=K_BLOCKS),
            )

        bias = held.tile([P, 1], F32, name="bias")
        nc.sync.dma_start(bias[:], b)

        identity = held.tile([P, P], BF16, name="identity")
        make_identity(nc, identity[:])

        zeros = held.tile([P, P], BF16, name="zeros")
        nc.vector.memset(zeros[:], 0.0)
        idle = psum.tile([P, WARM_REPEATS, P], F32, name="idle")
        for i in range(WARM_MATMULS):
            nc.tensor.matmul(
                idle[:],
                zeros[:],
                zeros[:].unsqueeze(1).to_broadcast([P, WARM_REPEATS, P]),
                start=True,
                stop=True,
            )

        warm = held.tile([P, 1], F32, name="warm")
        nc.vector.memset(warm[:], 0.0)
        nc.scalar.activation(warm[:], warm[:], TANH)

        features = [held.tile([P, S], BF16, name=f"features{c}") for c in range(K_BLOCKS)]
        for c in range(K_BLOCKS):
            for a in range(0, ROW_BLOCKS, 2):
                flipped = flips.tile([P, 2, P], BF16, name="flipped")
                for i in range(2):
                    nc.tensor.transpose(flipped[:, i, :], rows[:, a + i, c::K_BLOCKS], identity[:])
                nc.vector.tensor_copy(
                    features[c][:, a * P : (a + 2) * P], flipped[:].rearrange("p i s -> p (i s)")
                )

        acc = psum.tile([P, V], F32, name="acc")
        steps = [(c, t) for c in range(K_BLOCKS) for t in range(D)]
        for i, (c, t) in enumerate(steps):
            piece = offsets[:, t * PIECE_COLS : (t + 1) * PIECE_COLS]
            nc.tensor.matmul(
                acc[:],
                weights[:, t, c, :],
                features[c][:].indirect(piece),
                start=(i == 0),
                stop=(i == len(steps) - 1),
            )

        result = held.tile([P, V], F32, name="result", align_bytes=DMA_GRID)
        nc.scalar.activation(result[:], acc[:], TANH, bias=bias[:, 0:1])
        for first in range(0, V, V // 2):
            nc.scalar.dma_start(out[:, first : first + V // 2], result[:, first : first + V // 2])
